import numpy as np
import ml_dtypes


def mxq(x, axis, fmt="e4m3"):
    dtype, down = {"e4m3": (ml_dtypes.float8_e4m3fn, 7), "e5m2": (ml_dtypes.float8_e5m2, 14)}[fmt]
    v = np.moveaxis(np.asarray(x, np.float32).astype(ml_dtypes.bfloat16).astype(np.float64), axis, -1)
    blocks = v.reshape(v.shape[:-1] + (-1, 32))
    amax = np.abs(blocks).max(-1, keepdims=True)
    byte = np.maximum(np.where(amax > 0, np.frexp(amax)[1] - 1 + 127, 0) - down, 1)
    scale = np.exp2(byte - 127.0)
    codes = (blocks / scale).astype(np.float32).astype(dtype).astype(np.float64)
    return np.moveaxis((codes * scale).reshape(v.shape), -1, axis)


WIDE = False


def mx_kscale(k):
    if not WIDE:
        return np.ones(k)
    levels = np.array([10, -10, 5, -5, 0])
    if k % 512:
        return np.exp2(np.random.permutation(np.resize(levels, k // 32))).repeat(32)
    a = np.empty((k // 512, 16))
    for p in range(k // 512):
        a[p, :8] = np.random.permutation(np.resize(levels, 8))
        for g in range(8):
            far = levels[np.abs(levels - a[p, g]) >= 10]
            a[p, g + 8] = far[np.random.randint(len(far))]
    return np.exp2(a.ravel()).repeat(32)


def f64(x):
    return np.asarray(x).astype(np.float64)


def striped(idx):
    return np.tile(idx.reshape(-1, 16).T, (8, 1)).astype(np.uint16)


def unstriped(offs):
    return offs[:16].T.reshape(-1).astype(np.int64)


def relu2(v):
    return np.maximum(v, 0.0) ** 2


K, T, E, C, N = 512, 1280, 10, 256, 128
M = 512


def by_expert(wq, xq):
    return np.concatenate([wq[e].T @ xq[:, e * C:(e + 1) * C] for e in range(E)], axis=1)


def setup_inputs():
    n = np.random.standard_normal
    s = mx_kscale(K)[:, None]
    first = np.random.permutation(np.repeat(np.arange(E), T // E))
    second = (first + 1 + np.random.permutation(np.repeat(np.arange(E - 1), -(-T // (E - 1)))[:T])) % E
    while np.bincount(second, minlength=E).max() != T // E:
        load = np.bincount(second, minlength=E); hi, lo = int(load.argmax()), int(load.argmin())
        t = np.flatnonzero((second == hi) & (first != lo))[0]; second[t] = lo
    slot_token = np.empty(E * C, np.int64); pos = np.empty((2, T), np.int64); fill = np.zeros(E, np.int64)
    place = np.stack([np.random.permutation(C) for _ in range(E)])
    for r, deal in enumerate((first, second)):
        for t in np.random.permutation(T):
            e = deal[t]; j = e * C + place[e, fill[e]]; fill[e] += 1; slot_token[j] = t; pos[r, t] = j
    g = np.random.uniform(0.2, 0.8, T)
    r = mx_kscale(M)[:, None]
    return {
        "uT": (n((M, T)) * r).astype(np.float32),
        "wu": (n((M, K)) / np.sqrt(M) / r * s.T).astype(np.float32),
        "w": (n((E, K, N)) / np.sqrt(K) / s[None]).astype(np.float32),
        "b": (0.3 * n((N, E))).astype(np.float32),
        "gate": np.stack([np.tile(g, (N, 1)), np.tile(1.0 - g, (N, 1))]).astype(np.float32),
        "offs": striped(slot_token),
        "pos1": striped(pos[0]),
        "pos2": striped(pos[1]),
    }


def reference(uT, wu, w, b, gate, offs, pos1, pos2):
    idx = unstriped(offs)
    x = mxq(f64(wu), 0, "e4m3").T @ mxq(f64(uT), 0, "e4m3")
    xq = mxq(x[:, idx], 0, "e4m3")
    y = by_expert(mxq(f64(w), 1, "e4m3"), xq)
    y = relu2(y + np.repeat(f64(b), C, axis=1))
    return f64(gate[0]) * y[:, unstriped(pos1)] + f64(gate[1]) * y[:, unstriped(pos2)]

@@ -1,0 +1,216 @@
+from contextlib import ExitStack
+
+import concourse.mybir as mybir
+
+K, T, E, C, N, M = 512, 1280, 10, 256, 128, 512
+S = E * C
+FLOPS = 2 * M * K * T + 2 * K * N * S
+
+F32 = mybir.dt.float32
+BF16 = mybir.dt.bfloat16
+U32 = mybir.dt.uint32
+U16 = mybir.dt.uint16
+U8 = mybir.dt.uint8
+FP8X4 = mybir.dt.float8_e4m3fn_x4
+ACT = mybir.ActivationFunctionType
+ALU = mybir.AluOpType
+
+P = 128
+PACK = 4
+BANK = 512
+LIST_COL = 16
+LOADS = ["wua","u0","wub","u1","u2","u3","u4a","u4b"]
+CHUNKS = {"u0": (0, 256), "u1": (256, 256), "u2": (512, 256), "u3": (768, 256), "u4a": (1024, 128), "u4b": (1152, 128)}
+WU_ON_VECTOR = 104
+SLOT_GROUPS = [[0,2],[2,2],[4,2],[6,2],[8,1],[9,1]]
+ORDER = ["r0","r1","r2","w0","g0","i0","r3","w1","g1","i1","r4","w2","q0","g2","i2","w3","q1","g3","i3","w4","q2","g4","i4","q3","g5","i5","q4","q5","a0","s0","a1","s1","a2","s2","a3","s3","a4","s4","a5","s5"]
+OUT_CHUNKS = [[0,512],[512,384],[896,256],[1152,128]]
+
+
+def tile_moe_prv_lin_relu2_kernel(tc, uT, wu, w, b, gate, offs, pos1, pos2, out):
+    nc = tc.nc
+    with ExitStack() as ctx:
+        keep = ctx.enter_context(tc.tile_pool(name="keep", bufs=1))
+        proj_psum = ctx.enter_context(tc.psum_pool(name="proj_psum", bufs=4))
+        expert_psum = ctx.enter_context(tc.psum_pool(name="expert_psum", bufs=4))
+
+        def gp_copy(out, in_):
+            nc.gpsimd.tensor_scalar(out, in_, 1.0, 0.0, ALU.mult, ALU.add)
+
+        copies = {"V": nc.vector.tensor_copy, "S": nc.scalar.copy, "G": gp_copy}
+
+        def quantize(values, name):
+            width = values.shape[1] // PACK
+            codes = keep.tile([P, width], U32, name=name + "_codes", align_bytes=64)
+            scales = keep.tile([P, width], U8, name=name + "_scales", align_bytes=64)
+            nc.vector.quantize_mx(out=codes[:].bitcast(FP8X4), scales=scales[:], in_=values)
+            return codes, scales
+
+        def matmul(acc, lhs, lhs_cols, rhs, rhs_cols):
+            nc.tensor.matmul_mx(
+                out=acc,
+                lhsT=lhs[0][:, lhs_cols].bitcast(FP8X4),
+                lhsT_scale=lhs[1][:, lhs_cols],
+                rhs=rhs[0][:, rhs_cols].bitcast(FP8X4),
+                rhs_scale=rhs[1][:, rhs_cols],
+                start=True,
+                stop=True,
+            )
+
+        wu_raw = keep.tile([P, PACK, K], F32, name="wu_raw")
+        wu_rows = wu.rearrange("(p j) c -> p j c", j=PACK)
+        u_rows = uT.rearrange("(p j) t -> p j t", j=PACK)
+        u_raw = {}
+        for name in LOADS:
+            if name in CHUNKS:
+                start, width = CHUNKS[name]
+                raw = keep.tile([P, PACK, width], F32, name="raw_" + name)
+                nc.sync.dma_start(out=raw[:], in_=u_rows[:, :, start:start + width])
+                u_raw[name] = raw
+            else:
+                cols = {"wu": slice(0, K), "wua": slice(0, K // 2), "wub": slice(K // 2, K)}[name]
+                nc.sync.dma_start(out=wu_raw[:, :, cols], in_=wu_rows[:, :, cols])
+        slot_tokens = keep.tile([P, S // LIST_COL], U16, name="slot_tokens")
+        nc.sync.dma_start(slot_tokens[:], offs)
+        bias = keep.tile([P, E], F32, name="bias")
+        nc.sync.dma_start(out=bias[:], in_=b)
+        w_rows = w.rearrange("e (p j) n -> p e (j n)", j=PACK)
+        w_raw = []
+        for pair in range(E // 2):
+            raw = keep.tile([P, 2, PACK * N], F32, name="w_raw%d" % pair)
+            nc.sync.dma_start(out=raw[:], in_=w_rows[:, 2 * pair:2 * pair + 2, :])
+            w_raw.append(raw)
+        first_slot = keep.tile([P, T // LIST_COL], U16, name="first_slot")
+        nc.sync.dma_start(first_slot[:], pos1)
+        second_slot = keep.tile([P, T // LIST_COL], U16, name="second_slot")
+        nc.sync.dma_start(second_slot[:], pos2)
+        gates = keep.tile([P, 2, T], F32, name="gates")
+        nc.sync.dma_start(out=gates[:], in_=gate.rearrange("r p t -> p r t"))
+
+        zero_in = keep.tile([P, 1], F32, name="zero_in")
+        nc.vector.memset(zero_in[:], 0.0)
+        zero = keep.tile([P, 1], F32, name="zero")
+        nc.scalar.activation(zero[:], zero_in[:], ACT.Square)
+
+        wu_bf = keep.tile([P, PACK * K], BF16, name="wu_bf", align_bytes=64)
+        wu_dst = wu_bf[:].rearrange("p (t m j) -> p m t j", t=PACK, j=PACK)
+        wu_src = wu_raw[:].rearrange("p j (m t) -> p m t j", t=PACK)
+        nc.vector.tensor_copy(out=wu_dst[:, :P // 2], in_=wu_src[:, :P // 2])
+        nc.vector.tensor_copy(out=wu_dst[:, P // 2:WU_ON_VECTOR], in_=wu_src[:, P // 2:WU_ON_VECTOR])
+        nc.scalar.copy(out=wu_dst[:, WU_ON_VECTOR:], in_=wu_src[:, WU_ON_VECTOR:])
+        wu_q = quantize(wu_bf[:], "wu")
+
+        pairs = keep.tile([P, 2 * 2 * T], BF16, name="pairs", align_bytes=64)
+        pairs_by_half = pairs[:].rearrange("p (h n e) -> p h n e", h=2, e=2)
+        windows = [pairs[:, 2 * h * T:2 * (h + 1) * T].bitcast(U32) for h in range(2)]
+
+        def project(name, round_on, planes, copy_on):
+            start, width = CHUNKS[name]
+            u_bf = keep.tile([P, PACK * width], BF16, name="u_bf" + name, align_bytes=64, tag="ring_w", bufs=2)
+            copies[round_on](
+                out=u_bf[:].rearrange("p (c i j) -> p c j i", i=4, j=PACK),
+                in_=u_raw[name][:].rearrange("p j (c i) -> p c j i", i=4),
+            )
+            u_q = quantize(u_bf[:], name)
+            for t0, engine in zip(range(0, PACK, planes), copy_on):
+                acc = proj_psum.tile([P, planes, width], F32, name="proj")
+                for t in range(t0, t0 + planes):
+                    matmul(acc[:, t - t0, :], wu_q, slice(t * P, (t + 1) * P), u_q, slice(0, width))
+                copies[engine](
+                    out=pairs_by_half[:, t0 // 2:(t0 + planes) // 2, start:start + width, :],
+                    in_=acc[:].rearrange("p (h e) n -> p h n e", e=2),
+                )
+
+        project("u0", "V", 2, "SS")
+        project("u1", "V", 2, "SS")
+        project("u2", "V", 2, "SV")
+        project("u3", "V", 2, "SS")
+        project("u4a", "V", 4, "S")
+        project("u4b", "V", 2, "VS")
+
+        y = keep.tile([P, S], F32, name="y")
+        held = {}
+        w_q = {}
+
+        def round_weights(g):
+            w_bf = keep.tile([P, 2 * N * PACK], BF16, name="w_bf", align_bytes=64, tag="ring_w", bufs=2)
+            for i in range(2):
+                copies["VSSSS"[g]](
+                    out=w_bf[:, i * N * PACK:(i + 1) * N * PACK].rearrange("p (c i j) -> p c j i", i=4, j=PACK),
+                    in_=w_raw[g][:, i, :].rearrange("p (j c i) -> p c j i", j=PACK, i=4),
+                )
+            held["w", g] = w_bf
+
+        def quantize_weights(g):
+            q = quantize(held["w", g][:], "w%d" % g)
+            for i in range(2):
+                w_q[2 * g + i] = (q, slice(i * N, (i + 1) * N))
+
+        def gather(g):
+            first, count = SLOT_GROUPS[g]
+            n = count * C
+            offsets = slot_tokens[:, first * C // LIST_COL:(first + count) * C // LIST_COL]
+            halves = keep.tile([P, PACK * n], BF16, name="halves", align_bytes=64, tag="ring_h", bufs=2)
+            for h in range(2):
+                if "SSSSVD"[g] == "D":
+                    dst = halves[:].bitcast(U32).rearrange("p (n h) -> p n h", h=2)[:, :, h]
+                else:
+                    dst = halves[:, 2 * h * n:2 * (h + 1) * n].bitcast(U32)
+                nc.vector.tensor_copy(dst, windows[h].indirect(offsets))
+            held["x", g] = halves
+
+        def interleave(g):
+            first, count = SLOT_GROUPS[g]
+            if "SSSSVD"[g] == "D":
+                return
+            x_bf = keep.tile([P, PACK * count * C], BF16, name="x_bf", align_bytes=64, tag="ring_x", bufs=9)
+            copies["SSSSVD"[g]](
+                out=x_bf[:].bitcast(F32).rearrange("p (n h) -> p n h", h=2),
+                in_=held["x", g][:].bitcast(F32).rearrange("p (h n) -> p n h", h=2),
+            )
+            held["x", g] = x_bf
+
+        def multiply(g):
+            first, count = SLOT_GROUPS[g]
+            x_q = quantize(held["x", g][:], "x%d" % g)
+            acc = expert_psum.tile([P, count * C], F32, name="expert_acc")
+            for e in range(first, first + count):
+                cols = slice((e - first) * C, (e - first + 1) * C)
+                matmul(acc[:, cols], w_q[e][0], w_q[e][1], x_q, cols)
+            held["acc", g] = acc
+
+        def rectify(g):
+            first, count = SLOT_GROUPS[g]
+            relu = keep.tile([P, count * C], F32, name="relu", align_bytes=64, tag="ring_r", bufs=9)
+            acc = held["acc", g]
+            for e in range(first, first + count):
+                cols = slice((e - first) * C, (e - first + 1) * C)
+                if "SSSSSV"[g] == "S":
+                    nc.scalar.activation(relu[:, cols], acc[:, cols], ACT.Relu, bias=bias[:, e:e + 1])
+                else:
+                    nc.vector.tensor_scalar(relu[:, cols], acc[:, cols], bias[:, e:e + 1], 0.0, ALU.add, ALU.max)
+            held["relu", g] = relu
+
+        def square(g):
+            first, count = SLOT_GROUPS[g]
+            relu = held["relu", g]
+            dst = y[:, first * C:(first + count) * C]
+            if "SVSSSV"[g] == "S":
+                nc.scalar.activation(dst, relu[:], ACT.Square, bias=zero[:])
+            else:
+                nc.vector.tensor_tensor(dst, relu[:], relu[:], ALU.mult)
+
+        steps = {"r": round_weights, "w": quantize_weights, "g": gather, "i": interleave, "q": multiply, "a": rectify, "s": square}
+        for step in ORDER:
+            steps[step[0]](int(step[1:]))
+
+        for start, width in OUT_CHUNKS:
+            made = []
+            for r, slots in enumerate((first_slot, second_slot)):
+                prod = keep.tile([P, width], F32, name="prod%d_%d" % (r, start))
+                offsets = slots[:, start // LIST_COL:(start + width) // LIST_COL]
+                nc.vector.tensor_tensor(prod[:], y[:].indirect(offsets), gates[:, r, start:start + width], ALU.mult)
+                made.append(prod)
+            total = keep.tile([P, width], F32, name="total%d" % start)
+            nc.vector.tensor_tensor(total[:], made[0][:], made[1][:], ALU.add)
+            nc.sync.dma_start(out=out[:, start:start + width], in_=total[:])

@@ -19,8 +19,8 @@ P = 128
 PACK = 4
 BANK = 512
 LIST_COL = 16
-LOADS = ["wua","u0","wub","u1","u2","u3","u4a","u4b"]
-CHUNKS = {"u0": (0, 256), "u1": (256, 256), "u2": (512, 256), "u3": (768, 256), "u4a": (1024, 128), "u4b": (1152, 128)}
+LOADS = ["wu",512,512,256]
+PIECES = [256,256,256,256,128,128]
 WU_ON_VECTOR = 104
 SLOT_GROUPS = [[0,2],[2,2],[4,2],[6,2],[8,1],[9,1]]
 ORDER = ["r0","r1","r2","w0","g0","i0","r3","w1","g1","i1","r4","w2","q0","g2","i2","w3","q1","g3","i3","w4","q2","g4","i4","q3","g5","i5","q4","q5","a0","s0","a1","s1","a2","s2","a3","s3","a4","s4","a5","s5"]
@@ -31,8 +31,8 @@ def tile_moe_prv_lin_relu2_kernel(tc, uT, wu, w, b, gate, offs, pos1, pos2, out)
     nc = tc.nc
     with ExitStack() as ctx:
         keep = ctx.enter_context(tc.tile_pool(name="keep", bufs=1))
-        proj_psum = ctx.enter_context(tc.psum_pool(name="proj_psum", bufs=4))
-        expert_psum = ctx.enter_context(tc.psum_pool(name="expert_psum", bufs=4))
+        proj_psum = ctx.enter_context(tc.psum_pool(name="psum", bufs=8))
+        expert_psum = proj_psum
 
         def gp_copy(out, in_):
             nc.gpsimd.tensor_scalar(out, in_, 1.0, 0.0, ALU.mult, ALU.add)
@@ -60,23 +60,24 @@ def tile_moe_prv_lin_relu2_kernel(tc, uT, wu, w, b, gate, offs, pos1, pos2, out)
         wu_raw = keep.tile([P, PACK, K], F32, name="wu_raw")
         wu_rows = wu.rearrange("(p j) c -> p j c", j=PACK)
         u_rows = uT.rearrange("(p j) t -> p j t", j=PACK)
-        u_raw = {}
+        u_raw = keep.tile([P, PACK, T], F32, name="u_raw")
+        loaded = 0
         for name in LOADS:
-            if name in CHUNKS:
-                start, width = CHUNKS[name]
-                raw = keep.tile([P, PACK, width], F32, name="raw_" + name)
-                nc.sync.dma_start(out=raw[:], in_=u_rows[:, :, start:start + width])
-                u_raw[name] = raw
+            if isinstance(name, int):
+                cols = slice(loaded, loaded + name)
+                nc.sync.dma_start(out=u_raw[:, :, cols], in_=u_rows[:, :, cols])
+                loaded += name
             else:
                 cols = {"wu": slice(0, K), "wua": slice(0, K // 2), "wub": slice(K // 2, K)}[name]
                 nc.sync.dma_start(out=wu_raw[:, :, cols], in_=wu_rows[:, :, cols])
         slot_tokens = keep.tile([P, S // LIST_COL], U16, name="slot_tokens")
-        nc.sync.dma_start(slot_tokens[:], offs)
         bias = keep.tile([P, E], F32, name="bias")
-        nc.sync.dma_start(out=bias[:], in_=b)
         w_rows = w.rearrange("e (p j) n -> p e (j n)", j=PACK)
         w_raw = []
         for pair in range(E // 2):
+            if pair == 1:
+                nc.sync.dma_start(slot_tokens[:], offs)
+                nc.sync.dma_start(out=bias[:], in_=b)
             raw = keep.tile([P, 2, PACK * N], F32, name="w_raw%d" % pair)
             nc.sync.dma_start(out=raw[:], in_=w_rows[:, 2 * pair:2 * pair + 2, :])
             w_raw.append(raw)
@@ -95,8 +96,7 @@ def tile_moe_prv_lin_relu2_kernel(tc, uT, wu, w, b, gate, offs, pos1, pos2, out)
         wu_bf = keep.tile([P, PACK * K], BF16, name="wu_bf", align_bytes=64)
         wu_dst = wu_bf[:].rearrange("p (t m j) -> p m t j", t=PACK, j=PACK)
         wu_src = wu_raw[:].rearrange("p j (m t) -> p m t j", t=PACK)
-        nc.vector.tensor_copy(out=wu_dst[:, :P // 2], in_=wu_src[:, :P // 2])
-        nc.vector.tensor_copy(out=wu_dst[:, P // 2:WU_ON_VECTOR], in_=wu_src[:, P // 2:WU_ON_VECTOR])
+        nc.vector.tensor_copy(out=wu_dst[:, :WU_ON_VECTOR], in_=wu_src[:, :WU_ON_VECTOR])
         nc.scalar.copy(out=wu_dst[:, WU_ON_VECTOR:], in_=wu_src[:, WU_ON_VECTOR:])
         wu_q = quantize(wu_bf[:], "wu")
 
@@ -104,29 +104,34 @@ def tile_moe_prv_lin_relu2_kernel(tc, uT, wu, w, b, gate, offs, pos1, pos2, out)
         pairs_by_half = pairs[:].rearrange("p (h n e) -> p h n e", h=2, e=2)
         windows = [pairs[:, 2 * h * T:2 * (h + 1) * T].bitcast(U32) for h in range(2)]
 
-        def project(name, round_on, planes, copy_on):
-            start, width = CHUNKS[name]
-            u_bf = keep.tile([P, PACK * width], BF16, name="u_bf" + name, align_bytes=64, tag="ring_w", bufs=2)
-            copies[round_on](
-                out=u_bf[:].rearrange("p (c i j) -> p c j i", i=4, j=PACK),
-                in_=u_raw[name][:].rearrange("p j (c i) -> p c j i", i=4),
-            )
-            u_q = quantize(u_bf[:], name)
-            for t0, engine in zip(range(0, PACK, planes), copy_on):
-                acc = proj_psum.tile([P, planes, width], F32, name="proj")
-                for t in range(t0, t0 + planes):
-                    matmul(acc[:, t - t0, :], wu_q, slice(t * P, (t + 1) * P), u_q, slice(0, width))
-                copies[engine](
-                    out=pairs_by_half[:, t0 // 2:(t0 + planes) // 2, start:start + width, :],
-                    in_=acc[:].rearrange("p (h e) n -> p h n e", e=2),
-                )
+        u_q = []
 
-        project("u0", "V", 2, "SS")
-        project("u1", "V", 2, "SS")
-        project("u2", "V", 2, "SV")
-        project("u3", "V", 2, "SS")
-        project("u4a", "V", 4, "S")
-        project("u4b", "V", 2, "VS")
+        def round_tokens(i):
+            start, width = sum(PIECES[:i]), PIECES[i]
+            u_bf = keep.tile([P, PACK * width], BF16, name="u_bf%d" % i, align_bytes=64, tag="ring_w", bufs=2)
+            copies["SVVVVV"[i]](
+                out=u_bf[:].rearrange("p (c i j) -> p c j i", i=4, j=PACK),
+                in_=u_raw[:, :, start:start + width].rearrange("p j (c i) -> p c j i", i=4),
+            )
+            u_q.append(quantize(u_bf[:], "u%d" % i))
+
+        def project(i, h):
+            start, width = sum(PIECES[:i]), PIECES[i]
+            acc = proj_psum.tile([P, 2 * width], F32, name="acc")
+            for e in range(2):
+                t = 2 * h + e
+                matmul(acc[:, e * width:(e + 1) * width], wu_q, slice(t * P, (t + 1) * P), u_q[i], slice(0, width))
+            copies[("SSSSSV", "SSSSVS")[h][i]](
+                out=pairs_by_half[:, h, start:start + width, :],
+                in_=acc[:].rearrange("p (e n) -> p n e", e=2),
+            )
+
+        for i in range(len(PIECES) + 6):
+            if i < len(PIECES):
+                round_tokens(i)
+                project(i, 0)
+            if i >= 6:
+                project(i - 6, 1)
 
         y = keep.tile([P, S], F32, name="y")
         held = {}
@@ -173,7 +178,7 @@ def tile_moe_prv_lin_relu2_kernel(tc, uT, wu, w, b, gate, offs, pos1, pos2, out)
         def multiply(g):
             first, count = SLOT_GROUPS[g]
             x_q = quantize(held["x", g][:], "x%d" % g)
-            acc = expert_psum.tile([P, count * C], F32, name="expert_acc")
+            acc = expert_psum.tile([P, count * C], F32, name="acc")
             for e in range(first, first + count):
                 cols = slice((e - first) * C, (e - first + 1) * C)
                 matmul(acc[:, cols], w_q[e][0], w_q[e][1], x_q, cols)

@@ -17,27 +17,40 @@ ALU = mybir.AluOpType
 
 P = 128
 PACK = 4
-BANK = 512
+LINE = 4
 LIST_COL = 16
-LOADS = ["wu",512,512,256]
-PIECES = [256,256,256,256,128,128]
-WU_ON_VECTOR = 104
-SLOT_GROUPS = [[0,2],[2,2],[4,2],[6,2],[8,1],[9,1]]
-ORDER = ["r0","r1","r2","w0","g0","i0","r3","w1","g1","i1","r4","w2","q0","g2","i2","w3","q1","g3","i3","w4","q2","g4","i4","q3","g5","i5","q4","q5","a0","s0","a1","s1","a2","s2","a3","s3","a4","s4","a5","s5"]
-OUT_CHUNKS = [[0,512],[512,384],[896,256],[1152,128]]
+PSUM_BANKS = 8
+
+TOKEN_PIECES = [256, 256, 256, 256, 128, 128]
+SLOT_GROUPS = [(0, 2), (2, 2), (4, 2), (6, 2), (8, 1), (9, 1)]
+WEIGHT_GROUPS = [(0, 2), (2, 4), (6, 4)]
+OUT_PIECES = [(0, 512), (512, 384), (896, 256), (1152, 128)]
+
+VECTOR_ROUNDS_TOKENS = {0, 3, 5}
+VECTOR_EMPTIES_HALF0 = {4}
+VECTOR_ROUNDS_WEIGHTS = {0}
+VECTOR_INTERLEAVES = {5}
+VECTOR_RECTIFIES = {3, 5}
+VECTOR_SQUARES = {5}
+
+GATHER_BUFS = 3
+QUANTISE_LAG = 3
 
 
 def tile_moe_prv_lin_relu2_kernel(tc, uT, wu, w, b, gate, offs, pos1, pos2, out):
     nc = tc.nc
     with ExitStack() as ctx:
         keep = ctx.enter_context(tc.tile_pool(name="keep", bufs=1))
-        proj_psum = ctx.enter_context(tc.psum_pool(name="psum", bufs=8))
-        expert_psum = proj_psum
+        psum = ctx.enter_context(tc.psum_pool(name="psum", bufs=PSUM_BANKS))
 
-        def gp_copy(out, in_):
-            nc.gpsimd.tensor_scalar(out, in_, 1.0, 0.0, ALU.mult, ALU.add)
+        def copy_on(vector):
+            return nc.vector.tensor_copy if vector else nc.scalar.copy
 
-        copies = {"V": nc.vector.tensor_copy, "S": nc.scalar.copy, "G": gp_copy}
+        def round_rows(vector, dst, rows):
+            copy_on(vector)(
+                out=dst.rearrange("p (c i j) -> p c j i", i=LINE, j=PACK),
+                in_=rows.rearrange("p j (c i) -> p c j i", i=LINE),
+            )
 
         def quantize(values, name):
             width = values.shape[1] // PACK
@@ -57,30 +70,30 @@ def tile_moe_prv_lin_relu2_kernel(tc, uT, wu, w, b, gate, offs, pos1, pos2, out)
                 stop=True,
             )
 
-        wu_raw = keep.tile([P, PACK, K], F32, name="wu_raw")
-        wu_rows = wu.rearrange("(p j) c -> p j c", j=PACK)
+        piece_start = [sum(TOKEN_PIECES[:i]) for i in range(len(TOKEN_PIECES))]
         u_rows = uT.rearrange("(p j) t -> p j t", j=PACK)
-        u_raw = keep.tile([P, PACK, T], F32, name="u_raw")
-        loaded = 0
-        for name in LOADS:
-            if isinstance(name, int):
-                cols = slice(loaded, loaded + name)
-                nc.sync.dma_start(out=u_raw[:, :, cols], in_=u_rows[:, :, cols])
-                loaded += name
-            else:
-                cols = {"wu": slice(0, K), "wua": slice(0, K // 2), "wub": slice(K // 2, K)}[name]
-                nc.sync.dma_start(out=wu_raw[:, :, cols], in_=wu_rows[:, :, cols])
+        w_rows = w.rearrange("e (p j) n -> p e j n", j=PACK)
+
+        def load_tokens(i):
+            raw = keep.tile([P, PACK, TOKEN_PIECES[i]], F32, name="u_raw%d" % i)
+            nc.sync.dma_start(out=raw[:], in_=u_rows[:, :, piece_start[i]:piece_start[i] + TOKEN_PIECES[i]])
+            return raw
+
+        def load_weight_pair(pair):
+            raw = keep.tile([P, 2, PACK, N], F32, name="w_raw%d" % pair)
+            nc.sync.dma_start(out=raw[:], in_=w_rows[:, 2 * pair:2 * pair + 2])
+            return raw
+
+        u_raw = [load_tokens(0)]
+        wu_raw = keep.tile([P, PACK, K], F32, name="wu_raw")
+        nc.sync.dma_start(out=wu_raw[:], in_=wu.rearrange("(p j) c -> p j c", j=PACK))
+        u_raw.extend(load_tokens(i) for i in range(1, len(TOKEN_PIECES)))
+        w_raw = [load_weight_pair(0)]
         slot_tokens = keep.tile([P, S // LIST_COL], U16, name="slot_tokens")
+        nc.sync.dma_start(slot_tokens[:], offs)
         bias = keep.tile([P, E], F32, name="bias")
-        w_rows = w.rearrange("e (p j) n -> p e (j n)", j=PACK)
-        w_raw = []
-        for pair in range(E // 2):
-            if pair == 1:
-                nc.sync.dma_start(slot_tokens[:], offs)
-                nc.sync.dma_start(out=bias[:], in_=b)
-            raw = keep.tile([P, 2, PACK * N], F32, name="w_raw%d" % pair)
-            nc.sync.dma_start(out=raw[:], in_=w_rows[:, 2 * pair:2 * pair + 2, :])
-            w_raw.append(raw)
+        nc.sync.dma_start(out=bias[:], in_=b)
+        w_raw.extend(load_weight_pair(pair) for pair in range(1, E // 2))
         first_slot = keep.tile([P, T // LIST_COL], U16, name="first_slot")
         nc.sync.dma_start(first_slot[:], pos1)
         second_slot = keep.tile([P, T // LIST_COL], U16, name="second_slot")
@@ -93,129 +106,119 @@ def tile_moe_prv_lin_relu2_kernel(tc, uT, wu, w, b, gate, offs, pos1, pos2, out)
         zero = keep.tile([P, 1], F32, name="zero")
         nc.scalar.activation(zero[:], zero_in[:], ACT.Square)
 
-        wu_bf = keep.tile([P, PACK * K], BF16, name="wu_bf", align_bytes=64)
-        wu_dst = wu_bf[:].rearrange("p (t m j) -> p m t j", t=PACK, j=PACK)
-        wu_src = wu_raw[:].rearrange("p j (m t) -> p m t j", t=PACK)
-        nc.vector.tensor_copy(out=wu_dst[:, :WU_ON_VECTOR], in_=wu_src[:, :WU_ON_VECTOR])
-        nc.scalar.copy(out=wu_dst[:, WU_ON_VECTOR:], in_=wu_src[:, WU_ON_VECTOR:])
-        wu_q = quantize(wu_bf[:], "wu")
+        wu_halves = wu_raw[:].rearrange("p j (m h e) -> p h m j e", h=2, e=2)
+        wu_bf = []
+        for h in range(2):
+            rounded = keep.tile([P, 2 * P * PACK], BF16, name="wu_bf%d" % h, align_bytes=64)
+            nc.vector.tensor_copy(out=rounded[:].rearrange("p (e m j) -> p m j e", e=2, j=PACK), in_=wu_halves[:, h])
+            wu_bf.append(rounded)
+        wu_q = [quantize(wu_bf[h][:], "wu%d" % h) for h in range(2)]
 
-        pairs = keep.tile([P, 2 * 2 * T], BF16, name="pairs", align_bytes=64)
-        pairs_by_half = pairs[:].rearrange("p (h n e) -> p h n e", h=2, e=2)
-        windows = [pairs[:, 2 * h * T:2 * (h + 1) * T].bitcast(U32) for h in range(2)]
-
+        x_pairs = keep.tile([P, 2 * T * 2], BF16, name="x_pairs", align_bytes=64)
+        windows = [x_pairs[:, 2 * h * T:2 * (h + 1) * T].bitcast(U32) for h in range(2)]
         u_q = []
 
-        def round_tokens(i):
-            start, width = sum(PIECES[:i]), PIECES[i]
-            u_bf = keep.tile([P, PACK * width], BF16, name="u_bf%d" % i, align_bytes=64, tag="ring_w", bufs=2)
-            copies["SVVVVV"[i]](
-                out=u_bf[:].rearrange("p (c i j) -> p c j i", i=4, j=PACK),
-                in_=u_raw[:, :, start:start + width].rearrange("p j (c i) -> p c j i", i=4),
-            )
-            u_q.append(quantize(u_bf[:], "u%d" % i))
-
         def project(i, h):
-            start, width = sum(PIECES[:i]), PIECES[i]
-            acc = proj_psum.tile([P, 2 * width], F32, name="acc")
+            start, width = piece_start[i], TOKEN_PIECES[i]
+            acc = psum.tile([P, 2 * width], F32, name="acc")
             for e in range(2):
-                t = 2 * h + e
-                matmul(acc[:, e * width:(e + 1) * width], wu_q, slice(t * P, (t + 1) * P), u_q[i], slice(0, width))
-            copies[("SSSSSV", "SSSSVS")[h][i]](
-                out=pairs_by_half[:, h, start:start + width, :],
-                in_=acc[:].rearrange("p (e n) -> p n e", e=2),
+                matmul(acc[:, e * width:(e + 1) * width], wu_q[h], slice(e * P, (e + 1) * P), u_q[i], slice(0, width))
+            copy_on(h == 0 and i in VECTOR_EMPTIES_HALF0)(
+                out=x_pairs[:].rearrange("p (h t e) -> p h t e", h=2, e=2)[:, h, start:start + width, :],
+                in_=acc[:].rearrange("p (e t) -> p t e", e=2),
             )
 
-        for i in range(len(PIECES) + 6):
-            if i < len(PIECES):
-                round_tokens(i)
-                project(i, 0)
-            if i >= 6:
-                project(i - 6, 1)
+        for i, width in enumerate(TOKEN_PIECES):
+            u_bf = keep.tile([P, PACK * width], BF16, name="u_bf%d" % i, align_bytes=64)
+            round_rows(i in VECTOR_ROUNDS_TOKENS, u_bf[:], u_raw[i][:])
+            u_q.append(quantize(u_bf[:], "u%d" % i))
+            project(i, 0)
+        for i in range(len(TOKEN_PIECES)):
+            project(i, 1)
 
         y = keep.tile([P, S], F32, name="y")
-        held = {}
         w_q = {}
+        gathered, x_bf, sums, relu = {}, {}, {}, {}
 
-        def round_weights(g):
-            w_bf = keep.tile([P, 2 * N * PACK], BF16, name="w_bf", align_bytes=64, tag="ring_w", bufs=2)
-            for i in range(2):
-                copies["VSSSS"[g]](
-                    out=w_bf[:, i * N * PACK:(i + 1) * N * PACK].rearrange("p (c i j) -> p c j i", i=4, j=PACK),
-                    in_=w_raw[g][:, i, :].rearrange("p (j c i) -> p c j i", j=PACK, i=4),
-                )
-            held["w", g] = w_bf
-
-        def quantize_weights(g):
-            q = quantize(held["w", g][:], "w%d" % g)
-            for i in range(2):
-                w_q[2 * g + i] = (q, slice(i * N, (i + 1) * N))
+        def prepare_weights(g):
+            first, count = WEIGHT_GROUPS[g]
+            w_bf = keep.tile([P, count * N * PACK], BF16, name="w_bf%d" % g, align_bytes=64)
+            for i in range(count):
+                e = first + i
+                round_rows(g in VECTOR_ROUNDS_WEIGHTS, w_bf[:, i * N * PACK:(i + 1) * N * PACK], w_raw[e // 2][:, e % 2])
+            quantised = quantize(w_bf[:], "w%d" % g)
+            for i in range(count):
+                w_q[first + i] = (quantised, slice(i * N, (i + 1) * N))
 
         def gather(g):
             first, count = SLOT_GROUPS[g]
-            n = count * C
+            slots = count * C
             offsets = slot_tokens[:, first * C // LIST_COL:(first + count) * C // LIST_COL]
-            halves = keep.tile([P, PACK * n], BF16, name="halves", align_bytes=64, tag="ring_h", bufs=2)
+            words = keep.tile([P, PACK * slots], BF16, name="gathered", align_bytes=64, bufs=GATHER_BUFS)
             for h in range(2):
-                if "SSSSVD"[g] == "D":
-                    dst = halves[:].bitcast(U32).rearrange("p (n h) -> p n h", h=2)[:, :, h]
-                else:
-                    dst = halves[:, 2 * h * n:2 * (h + 1) * n].bitcast(U32)
-                nc.vector.tensor_copy(dst, windows[h].indirect(offsets))
-            held["x", g] = halves
+                nc.vector.tensor_copy(words[:, 2 * h * slots:2 * (h + 1) * slots].bitcast(U32), windows[h].indirect(offsets))
+            gathered[g] = words
 
         def interleave(g):
-            first, count = SLOT_GROUPS[g]
-            if "SSSSVD"[g] == "D":
-                return
-            x_bf = keep.tile([P, PACK * count * C], BF16, name="x_bf", align_bytes=64, tag="ring_x", bufs=9)
-            copies["SSSSVD"[g]](
-                out=x_bf[:].bitcast(F32).rearrange("p (n h) -> p n h", h=2),
-                in_=held["x", g][:].bitcast(F32).rearrange("p (h n) -> p n h", h=2),
+            values = keep.tile([P, PACK * SLOT_GROUPS[g][1] * C], BF16, name="x_bf%d" % g, align_bytes=64)
+            copy_on(g in VECTOR_INTERLEAVES)(
+                out=values[:].bitcast(F32).rearrange("p (s h) -> p s h", h=2),
+                in_=gathered[g][:].bitcast(F32).rearrange("p (h s) -> p s h", h=2),
             )
-            held["x", g] = x_bf
+            x_bf[g] = values
 
         def multiply(g):
             first, count = SLOT_GROUPS[g]
-            x_q = quantize(held["x", g][:], "x%d" % g)
-            acc = expert_psum.tile([P, count * C], F32, name="acc")
-            for e in range(first, first + count):
-                cols = slice((e - first) * C, (e - first + 1) * C)
-                matmul(acc[:, cols], w_q[e][0], w_q[e][1], x_q, cols)
-            held["acc", g] = acc
+            x_q = quantize(x_bf[g][:], "x%d" % g)
+            acc = psum.tile([P, count * C], F32, name="acc")
+            for i in range(count):
+                cols = slice(i * C, (i + 1) * C)
+                matmul(acc[:, cols], *w_q[first + i], x_q, cols)
+            sums[g] = acc
 
         def rectify(g):
             first, count = SLOT_GROUPS[g]
-            relu = keep.tile([P, count * C], F32, name="relu", align_bytes=64, tag="ring_r", bufs=9)
-            acc = held["acc", g]
-            for e in range(first, first + count):
-                cols = slice((e - first) * C, (e - first + 1) * C)
-                if "SSSSSV"[g] == "S":
-                    nc.scalar.activation(relu[:, cols], acc[:, cols], ACT.Relu, bias=bias[:, e:e + 1])
+            values = keep.tile([P, count * C], F32, name="relu%d" % g, align_bytes=64)
+            for i in range(count):
+                cols = slice(i * C, (i + 1) * C)
+                expert_bias = bias[:, first + i:first + i + 1]
+                if g in VECTOR_RECTIFIES:
+                    nc.vector.tensor_scalar(values[:, cols], sums[g][:, cols], expert_bias, 0.0, ALU.add, ALU.max)
                 else:
-                    nc.vector.tensor_scalar(relu[:, cols], acc[:, cols], bias[:, e:e + 1], 0.0, ALU.add, ALU.max)
-            held["relu", g] = relu
+                    nc.scalar.activation(values[:, cols], sums[g][:, cols], ACT.Relu, bias=expert_bias)
+            relu[g] = values
 
         def square(g):
             first, count = SLOT_GROUPS[g]
-            relu = held["relu", g]
             dst = y[:, first * C:(first + count) * C]
-            if "SVSSSV"[g] == "S":
-                nc.scalar.activation(dst, relu[:], ACT.Square, bias=zero[:])
+            if g in VECTOR_SQUARES:
+                nc.vector.tensor_tensor(dst, relu[g][:], relu[g][:], ALU.mult)
             else:
-                nc.vector.tensor_tensor(dst, relu[:], relu[:], ALU.mult)
+                nc.scalar.activation(dst, relu[g][:], ACT.Square, bias=zero[:])
 
-        steps = {"r": round_weights, "w": quantize_weights, "g": gather, "i": interleave, "q": multiply, "a": rectify, "s": square}
-        for step in ORDER:
-            steps[step[0]](int(step[1:]))
+        groups = len(SLOT_GROUPS)
+        for step in range(groups + QUANTISE_LAG):
+            if step >= QUANTISE_LAG:
+                multiply(step - QUANTISE_LAG)
+            if step < groups:
+                gather(step)
+            if step < len(WEIGHT_GROUPS):
+                prepare_weights(step)
+            if step < groups:
+                interleave(step)
+        rectify(0)
+        for g in range(1, groups):
+            rectify(g)
+            square(g - 1)
+        square(groups - 1)
 
-        for start, width in OUT_CHUNKS:
-            made = []
-            for r, slots in enumerate((first_slot, second_slot)):
-                prod = keep.tile([P, width], F32, name="prod%d_%d" % (r, start))
-                offsets = slots[:, start // LIST_COL:(start + width) // LIST_COL]
-                nc.vector.tensor_tensor(prod[:], y[:].indirect(offsets), gates[:, r, start:start + width], ALU.mult)
-                made.append(prod)
+        for start, width in OUT_PIECES:
+            products = []
+            for r, slot_list in enumerate((first_slot, second_slot)):
+                product = keep.tile([P, width], F32, name="product%d_%d" % (r, start))
+                offsets = slot_list[:, start // LIST_COL:(start + width) // LIST_COL]
+                nc.vector.tensor_tensor(product[:], y[:].indirect(offsets), gates[:, r, start:start + width], ALU.mult)
+                products.append(product)
             total = keep.tile([P, width], F32, name="total%d" % start)
-            nc.vector.tensor_tensor(total[:], made[0][:], made[1][:], ALU.add)
+            nc.vector.tensor_tensor(total[:], products[0][:], products[1][:], ALU.add)
             nc.sync.dma_start(out=out[:, start:start + width], in_=total[:])

from contextlib import ExitStack

import concourse.mybir as mybir

K, T, E, C, N, M = 512, 1280, 10, 256, 128, 512
S = E * C
FLOPS = 2 * M * K * T + 2 * K * N * S

F32 = mybir.dt.float32
BF16 = mybir.dt.bfloat16
U32 = mybir.dt.uint32
U16 = mybir.dt.uint16
U8 = mybir.dt.uint8
FP8X4 = mybir.dt.float8_e4m3fn_x4
ACT = mybir.ActivationFunctionType
ALU = mybir.AluOpType

P = 128
PACK = 4
LINE = 4
LIST_COL = 16
PSUM_BANKS = 8

TOKEN_PIECES = [256, 256, 256, 256, 128, 128]
SLOT_GROUPS = [(0, 2), (2, 2), (4, 2), (6, 2), (8, 1), (9, 1)]
WEIGHT_GROUPS = [(0, 2), (2, 4), (6, 4)]
OUT_PIECES = [(0, 512), (512, 384), (896, 256), (1152, 128)]

VECTOR_ROUNDS_TOKENS = {0, 3, 5}
VECTOR_EMPTIES_HALF0 = {4}
VECTOR_ROUNDS_WEIGHTS = {0}
VECTOR_INTERLEAVES = {5}
VECTOR_RECTIFIES = {3, 5}
VECTOR_SQUARES = {5}

GATHER_BUFS = 3
QUANTISE_LAG = 3


def tile_moe_prv_lin_relu2_kernel(tc, uT, wu, w, b, gate, offs, pos1, pos2, out):
    nc = tc.nc
    with ExitStack() as ctx:
        keep = ctx.enter_context(tc.tile_pool(name="keep", bufs=1))
        psum = ctx.enter_context(tc.psum_pool(name="psum", bufs=PSUM_BANKS))

        def copy_on(vector):
            return nc.vector.tensor_copy if vector else nc.scalar.copy

        def round_rows(vector, dst, rows):
            copy_on(vector)(
                out=dst.rearrange("p (c i j) -> p c j i", i=LINE, j=PACK),
                in_=rows.rearrange("p j (c i) -> p c j i", i=LINE),
            )

        def quantize(values, name):
            width = values.shape[1] // PACK
            codes = keep.tile([P, width], U32, name=name + "_codes", align_bytes=64)
            scales = keep.tile([P, width], U8, name=name + "_scales", align_bytes=64)
            nc.vector.quantize_mx(out=codes[:].bitcast(FP8X4), scales=scales[:], in_=values)
            return codes, scales

        def matmul(acc, lhs, lhs_cols, rhs, rhs_cols):
            nc.tensor.matmul_mx(
                out=acc,
                lhsT=lhs[0][:, lhs_cols].bitcast(FP8X4),
                lhsT_scale=lhs[1][:, lhs_cols],
                rhs=rhs[0][:, rhs_cols].bitcast(FP8X4),
                rhs_scale=rhs[1][:, rhs_cols],
                start=True,
                stop=True,
            )

        piece_start = [sum(TOKEN_PIECES[:i]) for i in range(len(TOKEN_PIECES))]
        u_rows = uT.rearrange("(p j) t -> p j t", j=PACK)
        w_rows = w.rearrange("e (p j) n -> p e j n", j=PACK)

        def load_tokens(i):
            raw = keep.tile([P, PACK, TOKEN_PIECES[i]], F32, name="u_raw%d" % i)
            nc.sync.dma_start(out=raw[:], in_=u_rows[:, :, piece_start[i]:piece_start[i] + TOKEN_PIECES[i]])
            return raw

        def load_weight_pair(pair):
            raw = keep.tile([P, 2, PACK, N], F32, name="w_raw%d" % pair)
            nc.sync.dma_start(out=raw[:], in_=w_rows[:, 2 * pair:2 * pair + 2])
            return raw

        u_raw = [load_tokens(0)]
        wu_raw = keep.tile([P, PACK, K], F32, name="wu_raw")
        nc.sync.dma_start(out=wu_raw[:], in_=wu.rearrange("(p j) c -> p j c", j=PACK))
        u_raw.extend(load_tokens(i) for i in range(1, len(TOKEN_PIECES)))
        w_raw = [load_weight_pair(0)]
        slot_tokens = keep.tile([P, S // LIST_COL], U16, name="slot_tokens")
        nc.sync.dma_start(slot_tokens[:], offs)
        bias = keep.tile([P, E], F32, name="bias")
        nc.sync.dma_start(out=bias[:], in_=b)
        w_raw.extend(load_weight_pair(pair) for pair in range(1, E // 2))
        first_slot = keep.tile([P, T // LIST_COL], U16, name="first_slot")
        nc.sync.dma_start(first_slot[:], pos1)
        second_slot = keep.tile([P, T // LIST_COL], U16, name="second_slot")
        nc.sync.dma_start(second_slot[:], pos2)
        gates = keep.tile([P, 2, T], F32, name="gates")
        nc.sync.dma_start(out=gates[:], in_=gate.rearrange("r p t -> p r t"))

        zero_in = keep.tile([P, 1], F32, name="zero_in")
        nc.vector.memset(zero_in[:], 0.0)
        zero = keep.tile([P, 1], F32, name="zero")
        nc.scalar.activation(zero[:], zero_in[:], ACT.Square)

        wu_halves = wu_raw[:].rearrange("p j (m h e) -> p h m j e", h=2, e=2)
        wu_bf = []
        for h in range(2):
            rounded = keep.tile([P, 2 * P * PACK], BF16, name="wu_bf%d" % h, align_bytes=64)
            nc.vector.tensor_copy(out=rounded[:].rearrange("p (e m j) -> p m j e", e=2, j=PACK), in_=wu_halves[:, h])
            wu_bf.append(rounded)
        wu_q = [quantize(wu_bf[h][:], "wu%d" % h) for h in range(2)]

        x_pairs = keep.tile([P, 2 * T * 2], BF16, name="x_pairs", align_bytes=64)
        windows = [x_pairs[:, 2 * h * T:2 * (h + 1) * T].bitcast(U32) for h in range(2)]
        u_q = []

        def project(i, h):
            start, width = piece_start[i], TOKEN_PIECES[i]
            acc = psum.tile([P, 2 * width], F32, name="acc")
            for e in range(2):
                matmul(acc[:, e * width:(e + 1) * width], wu_q[h], slice(e * P, (e + 1) * P), u_q[i], slice(0, width))
            copy_on(h == 0 and i in VECTOR_EMPTIES_HALF0)(
                out=x_pairs[:].rearrange("p (h t e) -> p h t e", h=2, e=2)[:, h, start:start + width, :],
                in_=acc[:].rearrange("p (e t) -> p t e", e=2),
            )

        for i, width in enumerate(TOKEN_PIECES):
            u_bf = keep.tile([P, PACK * width], BF16, name="u_bf%d" % i, align_bytes=64)
            round_rows(i in VECTOR_ROUNDS_TOKENS, u_bf[:], u_raw[i][:])
            u_q.append(quantize(u_bf[:], "u%d" % i))
            project(i, 0)
        for i in range(len(TOKEN_PIECES)):
            project(i, 1)

        y = keep.tile([P, S], F32, name="y")
        w_q = {}
        gathered, x_bf, sums, relu = {}, {}, {}, {}

        def prepare_weights(g):
            first, count = WEIGHT_GROUPS[g]
            w_bf = keep.tile([P, count * N * PACK], BF16, name="w_bf%d" % g, align_bytes=64)
            for i in range(count):
                e = first + i
                round_rows(g in VECTOR_ROUNDS_WEIGHTS, w_bf[:, i * N * PACK:(i + 1) * N * PACK], w_raw[e // 2][:, e % 2])
            quantised = quantize(w_bf[:], "w%d" % g)
            for i in range(count):
                w_q[first + i] = (quantised, slice(i * N, (i + 1) * N))

        def gather(g):
            first, count = SLOT_GROUPS[g]
            slots = count * C
            offsets = slot_tokens[:, first * C // LIST_COL:(first + count) * C // LIST_COL]
            words = keep.tile([P, PACK * slots], BF16, name="gathered", align_bytes=64, bufs=GATHER_BUFS)
            for h in range(2):
                nc.vector.tensor_copy(words[:, 2 * h * slots:2 * (h + 1) * slots].bitcast(U32), windows[h].indirect(offsets))
            gathered[g] = words

        def interleave(g):
            values = keep.tile([P, PACK * SLOT_GROUPS[g][1] * C], BF16, name="x_bf%d" % g, align_bytes=64)
            copy_on(g in VECTOR_INTERLEAVES)(
                out=values[:].bitcast(F32).rearrange("p (s h) -> p s h", h=2),
                in_=gathered[g][:].bitcast(F32).rearrange("p (h s) -> p s h", h=2),
            )
            x_bf[g] = values

        def multiply(g):
            first, count = SLOT_GROUPS[g]
            x_q = quantize(x_bf[g][:], "x%d" % g)
            acc = psum.tile([P, count * C], F32, name="acc")
            for i in range(count):
                cols = slice(i * C, (i + 1) * C)
                matmul(acc[:, cols], *w_q[first + i], x_q, cols)
            sums[g] = acc

        def rectify(g):
            first, count = SLOT_GROUPS[g]
            values = keep.tile([P, count * C], F32, name="relu%d" % g, align_bytes=64)
            for i in range(count):
                cols = slice(i * C, (i + 1) * C)
                expert_bias = bias[:, first + i:first + i + 1]
                if g in VECTOR_RECTIFIES:
                    nc.vector.tensor_scalar(values[:, cols], sums[g][:, cols], expert_bias, 0.0, ALU.add, ALU.max)
                else:
                    nc.scalar.activation(values[:, cols], sums[g][:, cols], ACT.Relu, bias=expert_bias)
            relu[g] = values

        def square(g):
            first, count = SLOT_GROUPS[g]
            dst = y[:, first * C:(first + count) * C]
            if g in VECTOR_SQUARES:
                nc.vector.tensor_tensor(dst, relu[g][:], relu[g][:], ALU.mult)
            else:
                nc.scalar.activation(dst, relu[g][:], ACT.Square, bias=zero[:])

        groups = len(SLOT_GROUPS)
        for step in range(groups + QUANTISE_LAG):
            if step >= QUANTISE_LAG:
                multiply(step - QUANTISE_LAG)
            if step < groups:
                gather(step)
            if step < len(WEIGHT_GROUPS):
                prepare_weights(step)
            if step < groups:
                interleave(step)
        rectify(0)
        for g in range(1, groups):
            rectify(g)
            square(g - 1)
        square(groups - 1)

        for start, width in OUT_PIECES:
            products = []
            for r, slot_list in enumerate((first_slot, second_slot)):
                product = keep.tile([P, width], F32, name="product%d_%d" % (r, start))
                offsets = slot_list[:, start // LIST_COL:(start + width) // LIST_COL]
                nc.vector.tensor_tensor(product[:], y[:].indirect(offsets), gates[:, r, start:start + width], ALU.mult)
                products.append(product)
            total = keep.tile([P, width], F32, name="total%d" % start)
            nc.vector.tensor_tensor(total[:], products[0][:], products[1][:], ALU.add)
            nc.sync.dma_start(out=out[:, start:start + width], in_=total[:])
